import numpy as np
import ml_dtypes


def mxq(x, axis, fmt="e4m3"):
    dtype, down = {"e4m3": (ml_dtypes.float8_e4m3fn, 7), "e5m2": (ml_dtypes.float8_e5m2, 14)}[fmt]
    v = np.moveaxis(np.asarray(x, np.float32).astype(ml_dtypes.bfloat16).astype(np.float64), axis, -1)
    blocks = v.reshape(v.shape[:-1] + (-1, 32))
    amax = np.abs(blocks).max(-1, keepdims=True)
    byte = np.maximum(np.where(amax > 0, np.frexp(amax)[1] - 1 + 127, 0) - down, 1)
    scale = np.exp2(byte - 127.0)
    codes = (blocks / scale).astype(np.float32).astype(dtype).astype(np.float64)
    return np.moveaxis((codes * scale).reshape(v.shape), -1, axis)


WIDE = False


def mx_kscale(k):
    if not WIDE:
        return np.ones(k)
    levels = np.array([10, -10, 5, -5, 0])
    if k % 512:
        return np.exp2(np.random.permutation(np.resize(levels, k // 32))).repeat(32)
    a = np.empty((k // 512, 16))
    for p in range(k // 512):
        a[p, :8] = np.random.permutation(np.resize(levels, 8))
        for g in range(8):
            far = levels[np.abs(levels - a[p, g]) >= 10]
            a[p, g + 8] = far[np.random.randint(len(far))]
    return np.exp2(a.ravel()).repeat(32)


def f64(x):
    return np.asarray(x).astype(np.float64)


def striped(idx):
    return np.tile(np.asarray(idx).reshape(-1, 16).T, (8, 1)).astype(np.uint16)


def unstriped(offs):
    return offs[:16].T.reshape(-1).astype(np.int64)


E2M1 = np.array([0.0, 0.5, 1.0, 1.5, 2.0, 3.0, 4.0, 6.0, -0.0, -0.5, -1.0, -1.5, -2.0, -3.0, -4.0, -6.0])


def pack_weight(w, fmt):
    k, n = w.shape
    w = f64(np.asarray(w, np.float32).astype(ml_dtypes.bfloat16)).reshape(k // 32, 32, n)
    amax = np.abs(w).max(1)
    if fmt == "e4m3":
        byte = np.frexp(amax)[1] - 1 + 127 - 7
    else:
        mant, ex = np.frexp(amax / 6.0)
        byte = np.where(mant > 0.5, ex, ex - 1) + 127
    byte = np.clip(np.where(amax > 0, byte, 1), 1, 254)
    scaled = (w * np.exp2(127.0 - byte)[:, None, :]).reshape(k, n).astype(np.float32)
    by_word = np.ascontiguousarray(scaled.reshape(k // 512, 128, 4, n).transpose(0, 1, 3, 2))
    if fmt == "e4m3":
        words = by_word.astype(ml_dtypes.float8_e4m3fn).view(np.uint8)
    else:
        c = by_word.astype(ml_dtypes.float4_e2m1fn).view(np.uint8) & 0xF
        words = (c[..., 0::2] | (c[..., 1::2] << 4)).reshape(k // 512, 128, 2 * n)
    return np.ascontiguousarray(words), np.ascontiguousarray(byte.astype(np.uint8).reshape(k // 512, 16, n))


def unpack_weight(words, scales, fmt):
    g, _, n = scales.shape
    words = np.ascontiguousarray(words).reshape(g, 128, n, -1)
    if fmt == "e4m3":
        vals = words.view(ml_dtypes.float8_e4m3fn).astype(np.float64)
    else:
        nib = np.empty((g, 128, n, 4), np.uint8)
        nib[..., 0::2] = words & 0xF
        nib[..., 1::2] = words >> 4
        vals = E2M1[nib]
    vals = vals * np.repeat(np.exp2(scales.astype(np.float64) - 127.0), 8, axis=1)[..., None]
    return vals.transpose(0, 1, 3, 2).reshape(g * 512, n)


def softplus(v):
    return np.log(1.0 + np.exp(v))


def bf(x):
    return np.asarray(x, np.float32).astype(ml_dtypes.bfloat16)


def planes(Y):
    r, m = Y.shape
    b = f64(bf(Y)).reshape(r // 32, 32, m)
    amax = np.abs(b).max(1)
    byte = np.clip(np.where(amax > 0, np.frexp(amax)[1] - 1 + 127 - 7, 1), 1, 254)
    codes = (b * np.exp2(127.0 - byte)[:, None, :]).reshape(r, m).astype(np.float32).astype(ml_dtypes.float8_e4m3fn).view(np.uint8)
    words = codes.reshape(r // 512, 128, 4, m).transpose(0, 1, 3, 2)
    return np.ascontiguousarray(words), np.ascontiguousarray(byte.astype(np.uint8).reshape(r // 512, 16, m))


K, L, T, J, N = 512, 512, 1024, 512, 512


def setup_inputs():
    n = np.random.standard_normal
    idx = np.random.permutation(T)[:J]
    fk = mx_kscale(K)
    fl = mx_kscale(L)
    xap = pack_weight(n((K, J)) / fk[:, None], "e4m3")
    xbp = pack_weight(n((L, J)) / fl[:, None], "e2m1")
    wbp = pack_weight(n((L, N)) * 1 / np.sqrt(L) * fl[:, None], "e4m3")
    return {
        "xa_words": xap[0],
        "xa_scales": xap[1],
        "wa": (n((K, N)) * 1 / np.sqrt(K) * fk[:, None]).astype(np.float32),
        "xb_words": xbp[0],
        "xb_scales": xbp[1],
        "wb_words": wbp[0],
        "wb_scales": wbp[1],
        "pr": (np.random.uniform(0.4, 2.0, (N, T))).astype(np.float32),
        "old": (1.0 * n((N, T))).astype(np.float32),
        "offs": striped(idx),
    }


def reference(xa_words, xa_scales, wa, xb_words, xb_scales, wb_words, wb_scales, pr, old, offs):
    idx = unstriped(offs)
    xau = unpack_weight(xa_words, xa_scales, "e4m3")
    xbu = unpack_weight(xb_words, xb_scales, "e2m1")
    wbu = unpack_weight(wb_words, wb_scales, "e4m3")
    waq = mxq(f64(wa), 0, "e4m3")
    v = waq.T @ xau
    u = wbu.T @ xbu
    s = softplus(u)
    sv = s * v
    num = np.zeros((N, T))
    num[:, idx] = sv
    den = np.zeros((N, T))
    den[:, idx] = s
    y = (num + f64(pr) * f64(old)) / (den + f64(pr))
    words, scales = planes(y)
    return y, words, scales

@@ -1,0 +1,293 @@
+import math
+from contextlib import ExitStack
+
+import concourse.mybir as mybir
+from concourse.masks import make_identity
+
+K, T, J, N = 512, 1024, 512, 512
+FLOPS = 2 * 2 * K * N * J
+
+F32 = mybir.dt.float32
+BF16 = mybir.dt.bfloat16
+I32 = mybir.dt.int32
+U32 = mybir.dt.uint32
+U16 = mybir.dt.uint16
+U8 = mybir.dt.uint8
+FP8X4 = mybir.dt.float8_e4m3fn_x4
+FP4X4 = mybir.dt.float4_e2m1fn_x4
+ACT = mybir.ActivationFunctionType
+ALU = mybir.AluOpType
+
+P = 128
+SLOTS = 4
+BANK = 512
+HALVES = T // BANK
+BLOCKS = BANK // P
+U_CAP = 30.0
+EXP_CAP = math.exp(U_CAP)
+
+
+def tile_list_weighted_writes_pl_kernel(
+    tc, xa_words, xa_scales, wa, xb_words, xb_scales, wb_words, wb_scales, pr, old, offs, out_0, out_1, out_2
+):
+    nc = tc.nc
+    with ExitStack() as ctx:
+        sb = ctx.enter_context(tc.tile_pool(name="sb", bufs=1))
+        ps = ctx.enter_context(tc.psum_pool(name="ps", bufs=1))
+
+        def sbuf(name, shape, dtype):
+            return sb.tile(shape, dtype, name=name, align_bytes=64)
+
+        offsets = sb.tile([P, J // 16], U16, name="offsets")
+        banks = [ps.tile([P, BANK], F32, name=f"bank{b}") for b in range(8)]
+        u_banks = banks[0:4]
+        v_bank = banks[4]
+        den_banks = banks[5:7]
+        num_banks = [banks[7], banks[0]]
+        y_banks = banks[1:3]
+        root_banks = banks[3:5]
+
+        wb_w = sbuf("wb_w", [P, N], U32)
+        wb_s = sbuf("wb_s", [P, N], U8)
+        wb_dw = sbuf("wb_dw", [P, N], U32)
+        wb_ds = sbuf("wb_ds", [P, N], U8)
+        xb_w = sbuf("xb_w", [P, 2 * J], U8)
+        xb_s = sbuf("xb_s", [P, J], U8)
+        xa_w = sbuf("xa_w", [P, J], U32)
+        xa_s = sbuf("xa_s", [P, J], U8)
+        wa_raw = sbuf("wa_raw", [P, 4, N], F32)
+        wa_bf = [sbuf(f"wa_bf{j}", [P, 4 * P], BF16)[:] for j in range(SLOTS)]
+        wa_w = sbuf("wa_w", [P, N], U32)
+        wa_s = sbuf("wa_s", [P, N], U8)
+        prior = [sbuf(f"prior{j}", [P, T], F32) for j in range(SLOTS)]
+        state = [sbuf(f"state{j}", [P, T], F32) for j in range(SLOTS)]
+        kept = [sbuf(f"kept{j}", [P, T], F32) for j in range(SLOTS)]
+        den_page = sbuf("den_page", [P, T], F32)
+        num_page = sbuf("num_page", [P, T], F32)
+        ident = sbuf("ident", [P, P], F32)
+        zero = sbuf("zero", [P, 1], F32)
+        one = sbuf("one", [P, 1], F32)
+        expu = [sbuf(f"expu{j}", [P, J], F32) for j in range(SLOTS)]
+        capped = [sbuf(f"capped{j}", [P, J], F32) for j in range(SLOTS)]
+        logs = [sbuf(f"logs{j}", [P, J], F32) for j in range(SLOTS)]
+        weight = sbuf("weight", [P, J], F32)
+        values = [sbuf(f"values{j}", [P, J], F32) for j in range(SLOTS)]
+        roots = [sbuf(f"root{i}", [P, T], F32) for i in range(2)]
+        recip = [sbuf(f"recip{i}", [P, T], F32) for i in range(2)]
+        turned = sbuf("turned", [P, T], F32)
+        y = sbuf("y", [P, 2, T], F32)
+        y_bf = [sbuf(f"y_bf{h}", [P, SLOTS * BANK], BF16) for h in range(HALVES)]
+        y_w = [sbuf(f"y_w{h}", [P, BANK], U32) for h in range(HALVES)]
+        y_s = sbuf("y_s", [P, T], U8)
+
+        def load_scales(plane, rows, quadrants=range(4)):
+            words = rows[0].bitcast(I32)
+            width = words.shape[1]
+            for q in quadrants:
+                nc.sync.dma_start(
+                    out=plane[32 * q : 32 * q + 32, :].bitcast(I32),
+                    in_=words[4 * q : 4 * q + 4, :].unsqueeze(0).to_broadcast([8, 4, width]),
+                )
+
+        def load_words(tile, words):
+            nc.sync.dma_start(out=tile[:].bitcast(I32), in_=words.bitcast(I32))
+
+        pr_rows = pr.rearrange("(p t) c -> p t c", t=SLOTS)
+        old_rows = old.rearrange("(p t) c -> p t c", t=SLOTS)
+        out_rows = out_0.rearrange("(p t) c -> p t c", t=SLOTS)
+
+        def load_page_rows(j):
+            nc.sync.dma_start(out=prior[j][:], in_=pr_rows[:, j, :])
+            nc.sync.dma_start(out=state[j][:], in_=old_rows[:, j, :])
+
+        load_scales(wb_s, wb_scales, range(0, 2))
+        load_words(wb_w, wb_words[0].rearrange("p n t -> p (n t)"))
+        load_words(xb_w, xb_words[0])
+        load_scales(wb_s, wb_scales, range(2, 4))
+        load_scales(xb_s, xb_scales)
+        nc.sync.dma_start(out=wa_raw[:], in_=wa.rearrange("(p i) n -> p i n", i=4))
+        load_words(xa_w, xa_words[0].rearrange("p n t -> p (n t)"))
+        load_scales(xa_s, xa_scales)
+        nc.sync.dma_start(offsets[:], offs)
+        for j in range(SLOTS):
+            load_page_rows(j)
+
+        nc.vector.memset(zero[:], 0.0)
+        nc.scalar.activation(one[:], zero[:], ACT.Exp)
+        nc.vector.memset(den_page[:], 0.0)
+        nc.vector.memset(num_page[:], 0.0)
+        make_identity(nc, ident[:])
+
+        def cols(j):
+            return slice(j * P, (j + 1) * P)
+
+        def half(h):
+            return slice(h * BANK, (h + 1) * BANK)
+
+        for j in range(SLOTS):
+            nc.vector.tensor_copy(out=wb_dw[:, cols(j)].bitcast(I32), in_=wb_w[:].bitcast(I32)[:, j::SLOTS])
+            nc.vector.tensor_copy(out=wb_ds[:, cols(j)], in_=wb_s[:, j::SLOTS])
+            nc.tensor.matmul_mx(
+                out=u_banks[j][:],
+                lhsT=wb_dw[:, cols(j)].bitcast(FP8X4),
+                lhsT_scale=wb_ds[:, cols(j)],
+                rhs=xb_w[:].bitcast(FP4X4),
+                rhs_scale=xb_s[:],
+                start=True,
+                stop=True,
+            )
+        for j in range(SLOTS):
+            nc.scalar.activation(expu[j][:], u_banks[j][:], ACT.Exp)
+            nc.vector.tensor_scalar(capped[j][:], expu[j][:], EXP_CAP, None, ALU.min)
+
+        def product(j):
+            return roots[(j + 1) % 2][:, 0:J]
+
+        def take_log(j):
+            nc.scalar.activation(logs[j][:], capped[j][:], ACT.Ln, bias=one[:])
+            if j > 0:
+                nc.scalar.activation(expu[j][:], u_banks[j][:], ACT.Relu, bias=-U_CAP)
+
+        def weigh_old(j):
+            nc.gpsimd.tensor_tensor(kept[j][:], prior[j][:], state[j][:], ALU.mult)
+
+        def quantise_wa(j):
+            cast = nc.vector.tensor_copy if j < 2 else nc.scalar.copy
+            cast(
+                out=wa_bf[j].rearrange("p (m i) -> p m i", i=4),
+                in_=wa_raw[:, :, j::SLOTS].rearrange("p i m -> p m i"),
+            )
+            nc.vector.quantize_mx(out=wa_w[:, cols(j)].bitcast(FP8X4), scales=wa_s[:, cols(j)], in_=wa_bf[j])
+
+        def make_values(j):
+            nc.tensor.matmul_mx(
+                out=v_bank[:],
+                lhsT=wa_w[:, cols(j)].bitcast(FP8X4),
+                lhsT_scale=wa_s[:, cols(j)],
+                rhs=xa_w[:].bitcast(FP8X4),
+                rhs_scale=xa_s[:],
+                start=True,
+                stop=True,
+            )
+            nc.scalar.copy(out=values[j][:], in_=v_bank[:])
+
+        def weigh_values(j):
+            nc.gpsimd.tensor_tensor(product(j), weight[:], values[j][:], ALU.mult)
+
+        def turn(bank, src, h, start, stop):
+            for b in range(BLOCKS):
+                nc.tensor.matmul(
+                    out=bank[:, cols(b)],
+                    lhsT=src[:, cols(h * BLOCKS + b)],
+                    rhs=ident[:],
+                    is_transpose=True,
+                    start=start and b == 0,
+                    stop=stop and b == BLOCKS - 1,
+                )
+
+        def open_sum(pair, first):
+            for h in range(HALVES):
+                turn(pair[h], first, h, True, False)
+
+        def close_sum(pair, second):
+            for h in range(HALVES):
+                turn(pair[h], second, h, False, True)
+
+        def make_weights(j):
+            if j == 0:
+                nc.vector.tensor_tensor(weight[:], u_banks[j][:], logs[j][:], ALU.max)
+            else:
+                nc.gpsimd.tensor_tensor(weight[:], expu[j][:], logs[j][:], ALU.add)
+
+        def place_weights(j):
+            nc.vector.tensor_copy(den_page[:].indirect(offsets[:]), weight[:])
+
+        def invert(j):
+            root = roots[j % 2]
+            for h in range(HALVES):
+                nc.scalar.activation(root[:, half(h)], den_banks[h][:], ACT.Abs_reciprocal_sqrt)
+            for h in range(HALVES):
+                if j < SLOTS - 1:
+                    nc.scalar.activation(recip[j % 2][:, half(h)], root[:, half(h)], ACT.Square)
+                else:
+                    turn(root_banks[h], root, h, True, True)
+                    nc.scalar.activation(recip[j % 2][:, half(h)], root_banks[h][:], ACT.Square)
+
+        def place_values(j):
+            nc.vector.tensor_copy(num_page[:].indirect(offsets[:]), product(j))
+
+        def divide_turned(j):
+            for h in range(HALVES):
+                nc.vector.tensor_tensor(turned[:, half(h)], num_banks[h][:], recip[j % 2][:, half(h)], ALU.mult)
+
+        def turn_back(j):
+            for h in range(HALVES):
+                turn(y_banks[h], turned, h, True, True)
+                nc.scalar.copy(out=y[:, j % 2, half(h)], in_=y_banks[h][:])
+            nc.sync.dma_start(out=out_rows[:, j, :], in_=y[:, j % 2, :])
+
+        def weave(copy, pair, h):
+            copy(
+                out=y_bf[h][:].rearrange("p (c t) -> p c t", t=SLOTS)[:, :, 2 * pair : 2 * pair + 2].rearrange(
+                    "p (c i) t -> p c t i", i=2
+                ),
+                in_=y[:, :, half(h)].rearrange("p t (c i) -> p c t i", i=2),
+            )
+
+        take_log(0)
+        make_weights(0)
+        place_weights(0)
+        quantise_wa(0)
+        make_values(0)
+        weigh_values(0)
+        take_log(1)
+        make_weights(1)
+        quantise_wa(1)
+        make_values(1)
+        weigh_old(0)
+        open_sum(den_banks, prior[0])
+        close_sum(den_banks, den_page)
+        open_sum(num_banks, kept[0])
+        for j in range(2, SLOTS):
+            take_log(j)
+        for j in range(2, SLOTS):
+            quantise_wa(j)
+        invert(0)
+        for j in range(2, SLOTS):
+            make_values(j)
+        for j in range(SLOTS - 1):
+            place_values(j)
+            open_sum(den_banks, prior[j + 1])
+            close_sum(num_banks, num_page)
+            place_weights(j + 1)
+            weigh_values(j + 1)
+            if j + 2 < SLOTS:
+                make_weights(j + 2)
+            weigh_old(j + 1)
+            divide_turned(j)
+            close_sum(den_banks, den_page)
+            invert(j + 1)
+            turn_back(j)
+            if j + 2 < SLOTS:
+                open_sum(num_banks, kept[j + 1])
+            if j == 1:
+                for h in range(HALVES):
+                    weave(nc.scalar.copy, 0, h)
+
+        last = SLOTS - 1
+        place_values(last)
+        words_out = out_1[0].rearrange("p c t -> p (c t)").bitcast(I32)
+        for h in range(HALVES):
+            nc.vector.tensor_tensor(turned[:, half(h)], num_page[:, half(h)], kept[last][:, half(h)], ALU.add)
+        for h in range(HALVES):
+            nc.vector.tensor_tensor(y[:, last % 2, half(h)], turned[:, half(h)], recip[last % 2][:, half(h)], ALU.mult)
+            nc.sync.dma_start(out=out_rows[:, last, half(h)], in_=y[:, last % 2, half(h)])
+        weave(nc.scalar.copy, 1, 0)
+        weave(nc.vector.tensor_copy, 1, 1)
+        for h in reversed(range(HALVES)):
+            nc.vector.quantize_mx(out=y_w[h][:].bitcast(FP8X4), scales=y_s[:, half(h)], in_=y_bf[h][:])
+            nc.sync.dma_start(out=words_out[:, half(h)], in_=y_w[h][:].bitcast(I32))
+        scales_out = out_2[0].bitcast(I32)
+        for q in range(4):
+            queue = nc.sync if q % 2 == 0 else nc.scalar
+            queue.dma_start(out=scales_out[4 * q : 4 * q + 4, :], in_=y_s[32 * q : 32 * q + 4, :].bitcast(I32))

@@ -22,6 +22,7 @@ P = 128
 SLOTS = 4
 BANK = 512
 HALVES = T // BANK
+QUARTERS = 4
 BLOCKS = BANK // P
 U_CAP = 30.0
 EXP_CAP = math.exp(U_CAP)
@@ -42,10 +43,9 @@ def tile_list_weighted_writes_pl_kernel(
         banks = [ps.tile([P, BANK], F32, name=f"bank{b}") for b in range(8)]
         u_banks = banks[0:4]
         v_bank = banks[4]
-        den_banks = banks[5:7]
-        num_banks = [banks[7], banks[0]]
-        y_banks = banks[1:3]
-        root_banks = banks[3:5]
+        den_banks = [banks[5:7]] * 3
+        num_banks = banks[1:3]
+        y_banks = [banks[7], banks[0]]
 
         wb_w = sbuf("wb_w", [P, N], U32)
         wb_s = sbuf("wb_s", [P, N], U8)
@@ -55,29 +55,33 @@ def tile_list_weighted_writes_pl_kernel(
         xb_s = sbuf("xb_s", [P, J], U8)
         xa_w = sbuf("xa_w", [P, J], U32)
         xa_s = sbuf("xa_s", [P, J], U8)
-        wa_raw = sbuf("wa_raw", [P, 4, N], F32)
-        wa_bf = [sbuf(f"wa_bf{j}", [P, 4 * P], BF16)[:] for j in range(SLOTS)]
+        wa_raw = [sbuf(f"wa_raw{h}", [P, 4, N // 2], F32) for h in range(2)]
+        head = sbuf("head", [P, 3 * J], F32)
+        wa_bf = head[:, 0 : 2 * J].bitcast(BF16)
         wa_w = sbuf("wa_w", [P, N], U32)
         wa_s = sbuf("wa_s", [P, N], U8)
         prior = [sbuf(f"prior{j}", [P, T], F32) for j in range(SLOTS)]
         state = [sbuf(f"state{j}", [P, T], F32) for j in range(SLOTS)]
-        kept = [sbuf(f"kept{j}", [P, T], F32) for j in range(SLOTS)]
-        den_page = sbuf("den_page", [P, T], F32)
+        kept = [None] + [sbuf(f"kept{j}", [P, T], F32) for j in range(1, SLOTS)]
+        den_pages = [sbuf(f"den_page{i}", [P, T], F32) for i in range(2)]
         num_page = sbuf("num_page", [P, T], F32)
         ident = sbuf("ident", [P, P], F32)
         zero = sbuf("zero", [P, 1], F32)
         one = sbuf("one", [P, 1], F32)
-        expu = [sbuf(f"expu{j}", [P, J], F32) for j in range(SLOTS)]
         capped = [sbuf(f"capped{j}", [P, J], F32) for j in range(SLOTS)]
-        logs = [sbuf(f"logs{j}", [P, J], F32) for j in range(SLOTS)]
-        weight = sbuf("weight", [P, J], F32)
-        values = [sbuf(f"values{j}", [P, J], F32) for j in range(SLOTS)]
+        expu = [sbuf(f"expu{j}", [P, J], F32)[:] for j in range(SLOTS - 1)] + [head[:, 2 * J : 3 * J]]
+        logs = [sbuf(f"logs{j}", [P, J], F32)[:] for j in range(SLOTS)]
+        logs[1] = kept[1][:, 0:J]
+        excess = [kept[j][:, J : 2 * J] for j in range(1, SLOTS)]
+        values = [sbuf(f"values{j}", [P, J], F32)[:] for j in range(2)] + [kept[j][:, 0:J] for j in range(2, SLOTS)]
         roots = [sbuf(f"root{i}", [P, T], F32) for i in range(2)]
-        recip = [sbuf(f"recip{i}", [P, T], F32) for i in range(2)]
-        turned = sbuf("turned", [P, T], F32)
+        recip = [sbuf(f"recip{i}", [P, T], F32) for i in range(SLOTS)]
+        turned = [sbuf("turned", [P, T], F32), recip[1]]
+        weights = [sbuf("first", [P, J], F32)[:], values[0], values[1], recip[1][:, J // 2 : J // 2 + J]]
+        kept_halves = [[head[:, 3 * J // 2 : 5 * J // 2], weights[0]]] + [[kept[j][:, 0:BANK], kept[j][:, BANK:T]] for j in range(1, SLOTS)]
         y = sbuf("y", [P, 2, T], F32)
-        y_bf = [sbuf(f"y_bf{h}", [P, SLOTS * BANK], BF16) for h in range(HALVES)]
-        y_w = [sbuf(f"y_w{h}", [P, BANK], U32) for h in range(HALVES)]
+        y_bf = [sbuf(f"y_bf{h}", [P, SLOTS * T // QUARTERS], BF16) for h in range(QUARTERS)]
+        y_w = sbuf("y_w", [P, T], U32)
         y_s = sbuf("y_s", [P, T], U8)
 
         def load_scales(plane, rows, quadrants=range(4)):
@@ -105,7 +109,8 @@ def tile_list_weighted_writes_pl_kernel(
         load_words(xb_w, xb_words[0])
         load_scales(wb_s, wb_scales, range(2, 4))
         load_scales(xb_s, xb_scales)
-        nc.sync.dma_start(out=wa_raw[:], in_=wa.rearrange("(p i) n -> p i n", i=4))
+        for h in range(2):
+            nc.sync.dma_start(out=wa_raw[h][:], in_=wa.rearrange("(p i) (h n) -> p h i n", i=4, h=2)[:, h])
         load_words(xa_w, xa_words[0].rearrange("p n t -> p (n t)"))
         load_scales(xa_s, xa_scales)
         nc.sync.dma_start(offsets[:], offs)
@@ -114,15 +119,19 @@ def tile_list_weighted_writes_pl_kernel(
 
         nc.vector.memset(zero[:], 0.0)
         nc.scalar.activation(one[:], zero[:], ACT.Exp)
-        nc.vector.memset(den_page[:], 0.0)
-        nc.vector.memset(num_page[:], 0.0)
+        for page in den_pages:
+            nc.vector.memset(page[:], 0.0)
         make_identity(nc, ident[:])
+        nc.gpsimd.memset(num_page[:], 0.0)
 
         def cols(j):
             return slice(j * P, (j + 1) * P)
 
         def half(h):
             return slice(h * BANK, (h + 1) * BANK)
+
+        def quarter(q):
+            return slice(q * T // QUARTERS, (q + 1) * T // QUARTERS)
 
         for j in range(SLOTS):
             nc.vector.tensor_copy(out=wb_dw[:, cols(j)].bitcast(I32), in_=wb_w[:].bitcast(I32)[:, j::SLOTS])
@@ -137,27 +146,35 @@ def tile_list_weighted_writes_pl_kernel(
                 stop=True,
             )
         for j in range(SLOTS):
-            nc.scalar.activation(expu[j][:], u_banks[j][:], ACT.Exp)
-            nc.vector.tensor_scalar(capped[j][:], expu[j][:], EXP_CAP, None, ALU.min)
+            nc.scalar.activation(expu[j], u_banks[j][:], ACT.Exp)
+
+        def cap(j):
+            nc.vector.tensor_scalar(capped[j][:], expu[j], EXP_CAP, None, ALU.min)
 
         def product(j):
-            return roots[(j + 1) % 2][:, 0:J]
+            return capped[0][:] if j == 0 else roots[(j + 1) % 2][:, 0:J]
+
 
         def take_log(j):
-            nc.scalar.activation(logs[j][:], capped[j][:], ACT.Ln, bias=one[:])
-            if j > 0:
-                nc.scalar.activation(expu[j][:], u_banks[j][:], ACT.Relu, bias=-U_CAP)
+            nc.scalar.activation(logs[j], capped[j][:], ACT.Ln, bias=one[:])
+
+        def take_excess(j):
+            nc.scalar.activation(excess[j - 1], u_banks[j][:], ACT.Relu, bias=-U_CAP)
 
         def weigh_old(j):
-            nc.gpsimd.tensor_tensor(kept[j][:], prior[j][:], state[j][:], ALU.mult)
+            if j == 0:
+                for h in range(HALVES):
+                    nc.gpsimd.tensor_tensor(kept_halves[0][h], prior[0][:, half(h)], state[0][:, half(h)], ALU.mult)
+            else:
+                nc.gpsimd.tensor_tensor(kept[j][:], prior[j][:], state[j][:], ALU.mult)
 
-        def quantise_wa(j):
-            cast = nc.vector.tensor_copy if j < 2 else nc.scalar.copy
-            cast(
-                out=wa_bf[j].rearrange("p (m i) -> p m i", i=4),
-                in_=wa_raw[:, :, j::SLOTS].rearrange("p i m -> p m i"),
-            )
-            nc.vector.quantize_mx(out=wa_w[:, cols(j)].bitcast(FP8X4), scales=wa_s[:, cols(j)], in_=wa_bf[j])
+        def quantise_wa():
+            for h in range(2):
+                nc.vector.tensor_copy(
+                    out=wa_bf.rearrange("p (t h m i) -> p h t m i", t=SLOTS, h=2, i=4)[:, h],
+                    in_=wa_raw[h][:].rearrange("p i (m t) -> p t m i", t=SLOTS),
+                )
+            nc.vector.quantize_mx(out=wa_w[:].bitcast(FP8X4), scales=wa_s[:], in_=wa_bf)
 
         def make_values(j):
             nc.tensor.matmul_mx(
@@ -169,16 +186,16 @@ def tile_list_weighted_writes_pl_kernel(
                 start=True,
                 stop=True,
             )
-            nc.scalar.copy(out=values[j][:], in_=v_bank[:])
+            nc.scalar.copy(out=values[j], in_=v_bank[:])
 
         def weigh_values(j):
-            nc.gpsimd.tensor_tensor(product(j), weight[:], values[j][:], ALU.mult)
+            nc.gpsimd.tensor_tensor(product(j), weights[j], values[j], ALU.mult)
 
-        def turn(bank, src, h, start, stop):
+        def turn(bank, src, start, stop):
             for b in range(BLOCKS):
                 nc.tensor.matmul(
                     out=bank[:, cols(b)],
-                    lhsT=src[:, cols(h * BLOCKS + b)],
+                    lhsT=src[:, cols(b)],
                     rhs=ident[:],
                     is_transpose=True,
                     start=start and b == 0,
@@ -187,106 +204,135 @@ def tile_list_weighted_writes_pl_kernel(
 
         def open_sum(pair, first):
             for h in range(HALVES):
-                turn(pair[h], first, h, True, False)
+                turn(pair[h], first[h], True, False)
 
         def close_sum(pair, second):
             for h in range(HALVES):
-                turn(pair[h], second, h, False, True)
+                turn(pair[h], second[:, half(h)], False, True)
 
         def make_weights(j):
             if j == 0:
-                nc.vector.tensor_tensor(weight[:], u_banks[j][:], logs[j][:], ALU.max)
+                nc.vector.tensor_tensor(weights[j], u_banks[j][:], logs[j], ALU.max)
             else:
-                nc.gpsimd.tensor_tensor(weight[:], expu[j][:], logs[j][:], ALU.add)
+                nc.gpsimd.tensor_tensor(weights[j], excess[j - 1], logs[j], ALU.add)
 
         def place_weights(j):
-            nc.vector.tensor_copy(den_page[:].indirect(offsets[:]), weight[:])
+            nc.vector.tensor_copy(den_pages[j % 2][:].indirect(offsets[:]), weights[j])
 
-        def invert(j):
-            root = roots[j % 2]
+        def take_roots(j):
             for h in range(HALVES):
-                nc.scalar.activation(root[:, half(h)], den_banks[h][:], ACT.Abs_reciprocal_sqrt)
+                nc.scalar.activation(roots[j % 2][:, half(h)], den_banks[j][h][:], ACT.Abs_reciprocal_sqrt)
+
+        def square_roots(j):
             for h in range(HALVES):
-                if j < SLOTS - 1:
-                    nc.scalar.activation(recip[j % 2][:, half(h)], root[:, half(h)], ACT.Square)
-                else:
-                    turn(root_banks[h], root, h, True, True)
-                    nc.scalar.activation(recip[j % 2][:, half(h)], root_banks[h][:], ACT.Square)
+                nc.scalar.activation(recip[j][:, half(h)], roots[j % 2][:, half(h)], ACT.Square)
 
         def place_values(j):
             nc.vector.tensor_copy(num_page[:].indirect(offsets[:]), product(j))
 
         def divide_turned(j):
             for h in range(HALVES):
-                nc.vector.tensor_tensor(turned[:, half(h)], num_banks[h][:], recip[j % 2][:, half(h)], ALU.mult)
+                nc.vector.tensor_tensor(turned[j // 2][:, half(h)], num_banks[h][:], recip[j][:, half(h)], ALU.mult)
 
         def turn_back(j):
             for h in range(HALVES):
-                turn(y_banks[h], turned, h, True, True)
+                turn(y_banks[h], turned[j // 2][:, half(h)], True, True)
                 nc.scalar.copy(out=y[:, j % 2, half(h)], in_=y_banks[h][:])
-            nc.sync.dma_start(out=out_rows[:, j, :], in_=y[:, j % 2, :])
+            nc.scalar.dma_start(out=out_rows[:, j, :], in_=y[:, j % 2, :])
 
         def weave(copy, pair, h):
             copy(
                 out=y_bf[h][:].rearrange("p (c t) -> p c t", t=SLOTS)[:, :, 2 * pair : 2 * pair + 2].rearrange(
                     "p (c i) t -> p c t i", i=2
                 ),
-                in_=y[:, :, half(h)].rearrange("p t (c i) -> p c t i", i=2),
+                in_=y[:, :, quarter(h)].rearrange("p t (c i) -> p c t i", i=2),
             )
 
+        cap(0)
         take_log(0)
         make_weights(0)
+        quantise_wa()
+        for j in range(1, SLOTS):
+            cap(j)
         place_weights(0)
-        quantise_wa(0)
         make_values(0)
         weigh_values(0)
         take_log(1)
+        take_excess(1)
+        place_values(0)
         make_weights(1)
-        quantise_wa(1)
         make_values(1)
         weigh_old(0)
-        open_sum(den_banks, prior[0])
-        close_sum(den_banks, den_page)
-        open_sum(num_banks, kept[0])
+        weigh_old(1)
+        open_sum(den_banks[0], [prior[0][:, half(h)] for h in range(HALVES)])
+        close_sum(den_banks[0], den_pages[0])
+        place_weights(1)
         for j in range(2, SLOTS):
             take_log(j)
         for j in range(2, SLOTS):
-            quantise_wa(j)
-        invert(0)
-        for j in range(2, SLOTS):
-            make_values(j)
-        for j in range(SLOTS - 1):
-            place_values(j)
-            open_sum(den_banks, prior[j + 1])
-            close_sum(num_banks, num_page)
-            place_weights(j + 1)
-            weigh_values(j + 1)
-            if j + 2 < SLOTS:
-                make_weights(j + 2)
-            weigh_old(j + 1)
-            divide_turned(j)
-            close_sum(den_banks, den_page)
-            invert(j + 1)
-            turn_back(j)
-            if j + 2 < SLOTS:
-                open_sum(num_banks, kept[j + 1])
-            if j == 1:
-                for h in range(HALVES):
-                    weave(nc.scalar.copy, 0, h)
+            take_excess(j)
+        take_roots(0)
+        square_roots(0)
+        make_values(2)
+        open_sum(num_banks, kept_halves[0])
+        close_sum(num_banks, num_page)
+        open_sum(den_banks[1], [prior[1][:, half(h)] for h in range(HALVES)])
+        make_values(3)
+        weigh_values(1)
+        make_weights(2)
+        divide_turned(0)
+        close_sum(den_banks[1], den_pages[1])
+        take_roots(1)
+        square_roots(1)
+        turn_back(0)
+        open_sum(num_banks, kept_halves[1])
+
+        place_values(1)
+        open_sum(den_banks[2], [prior[2][:, half(h)] for h in range(HALVES)])
+        close_sum(num_banks, num_page)
+        place_weights(2)
+        weigh_values(2)
+        weigh_old(2)
+        divide_turned(1)
+        make_weights(3)
+        close_sum(den_banks[2], den_pages[0])
+        take_roots(2)
+        square_roots(2)
+        turn_back(1)
+        open_sum(num_banks, kept_halves[2])
+        for q in range(QUARTERS):
+            weave(nc.scalar.copy, 0, q)
+
+        place_values(2)
+        close_sum(num_banks, num_page)
+        weigh_values(3)
+        weigh_old(3)
+        place_weights(3)
+        divide_turned(2)
+        for h in range(HALVES):
+            nc.gpsimd.tensor_tensor(state[3][:, half(h)], prior[3][:, half(h)], den_pages[1][:, half(h)], ALU.add)
+            nc.scalar.activation(y[:, 1, half(h)], state[3][:, half(h)], ACT.Abs_reciprocal_sqrt)
+            nc.scalar.activation(recip[3][:, half(h)], y[:, 1, half(h)], ACT.Square)
+        turn_back(2)
 
         last = SLOTS - 1
         place_values(last)
         words_out = out_1[0].rearrange("p c t -> p (c t)").bitcast(I32)
         for h in range(HALVES):
-            nc.vector.tensor_tensor(turned[:, half(h)], num_page[:, half(h)], kept[last][:, half(h)], ALU.add)
-        for h in range(HALVES):
-            nc.vector.tensor_tensor(y[:, last % 2, half(h)], turned[:, half(h)], recip[last % 2][:, half(h)], ALU.mult)
+            for q in (2 * h, 2 * h + 1):
+                nc.vector.tensor_tensor(
+                    turned[0][:, quarter(q % 2)], num_page[:, quarter(q)], kept[last][:, quarter(q)], ALU.add
+                )
+            for q in (2 * h, 2 * h + 1):
+                nc.vector.tensor_tensor(
+                    y[:, last % 2, quarter(q)], turned[0][:, quarter(q % 2)], recip[last][:, quarter(q)], ALU.mult
+                )
+                weave(nc.scalar.copy if q < QUARTERS - 1 else nc.vector.tensor_copy, 1, q)
             nc.sync.dma_start(out=out_rows[:, last, half(h)], in_=y[:, last % 2, half(h)])
-        weave(nc.scalar.copy, 1, 0)
-        weave(nc.vector.tensor_copy, 1, 1)
-        for h in reversed(range(HALVES)):
-            nc.vector.quantize_mx(out=y_w[h][:].bitcast(FP8X4), scales=y_s[:, half(h)], in_=y_bf[h][:])
-            nc.sync.dma_start(out=words_out[:, half(h)], in_=y_w[h][:].bitcast(I32))
+        for q in (0, 1, 3, 2):
+            nc.vector.quantize_mx(out=y_w[:, quarter(q)].bitcast(FP8X4), scales=y_s[:, quarter(q)], in_=y_bf[q][:])
+            if q in (1, 2):
+                nc.sync.dma_start(out=words_out[:, half(q // 2)], in_=y_w[:, half(q // 2)].bitcast(I32))
         scales_out = out_2[0].bitcast(I32)
         for q in range(4):
             queue = nc.sync if q % 2 == 0 else nc.scalar

import math
from contextlib import ExitStack

import concourse.mybir as mybir
from concourse.masks import make_identity

K, T, J, N = 512, 1024, 512, 512
FLOPS = 2 * 2 * K * N * J

F32 = mybir.dt.float32
BF16 = mybir.dt.bfloat16
I32 = mybir.dt.int32
U32 = mybir.dt.uint32
U16 = mybir.dt.uint16
U8 = mybir.dt.uint8
FP8X4 = mybir.dt.float8_e4m3fn_x4
FP4X4 = mybir.dt.float4_e2m1fn_x4
ACT = mybir.ActivationFunctionType
ALU = mybir.AluOpType

P = 128
SLOTS = 4
BANK = 512
HALVES = T // BANK
QUARTERS = 4
BLOCKS = BANK // P
U_CAP = 30.0
EXP_CAP = math.exp(U_CAP)


def tile_list_weighted_writes_pl_kernel(
    tc, xa_words, xa_scales, wa, xb_words, xb_scales, wb_words, wb_scales, pr, old, offs, out_0, out_1, out_2
):
    nc = tc.nc
    with ExitStack() as ctx:
        sb = ctx.enter_context(tc.tile_pool(name="sb", bufs=1))
        ps = ctx.enter_context(tc.psum_pool(name="ps", bufs=1))

        def sbuf(name, shape, dtype):
            return sb.tile(shape, dtype, name=name, align_bytes=64)

        offsets = sb.tile([P, J // 16], U16, name="offsets")
        banks = [ps.tile([P, BANK], F32, name=f"bank{b}") for b in range(8)]
        u_banks = banks[0:4]
        v_bank = banks[4]
        den_banks = [banks[5:7]] * 3
        num_banks = banks[1:3]
        y_banks = [banks[7], banks[0]]

        wb_w = sbuf("wb_w", [P, N], U32)
        wb_s = sbuf("wb_s", [P, N], U8)
        wb_dw = sbuf("wb_dw", [P, N], U32)
        wb_ds = sbuf("wb_ds", [P, N], U8)
        xb_w = sbuf("xb_w", [P, 2 * J], U8)
        xb_s = sbuf("xb_s", [P, J], U8)
        xa_w = sbuf("xa_w", [P, J], U32)
        xa_s = sbuf("xa_s", [P, J], U8)
        wa_raw = [sbuf(f"wa_raw{h}", [P, 4, N // 2], F32) for h in range(2)]
        head = sbuf("head", [P, 3 * J], F32)
        wa_bf = head[:, 0 : 2 * J].bitcast(BF16)
        wa_w = sbuf("wa_w", [P, N], U32)
        wa_s = sbuf("wa_s", [P, N], U8)
        prior = [sbuf(f"prior{j}", [P, T], F32) for j in range(SLOTS)]
        state = [sbuf(f"state{j}", [P, T], F32) for j in range(SLOTS)]
        kept = [None] + [sbuf(f"kept{j}", [P, T], F32) for j in range(1, SLOTS)]
        den_pages = [sbuf(f"den_page{i}", [P, T], F32) for i in range(2)]
        num_page = sbuf("num_page", [P, T], F32)
        ident = sbuf("ident", [P, P], F32)
        zero = sbuf("zero", [P, 1], F32)
        one = sbuf("one", [P, 1], F32)
        capped = [sbuf(f"capped{j}", [P, J], F32) for j in range(SLOTS)]
        expu = [sbuf(f"expu{j}", [P, J], F32)[:] for j in range(SLOTS - 1)] + [head[:, 2 * J : 3 * J]]
        logs = [sbuf(f"logs{j}", [P, J], F32)[:] for j in range(SLOTS)]
        logs[1] = kept[1][:, 0:J]
        excess = [kept[j][:, J : 2 * J] for j in range(1, SLOTS)]
        values = [sbuf(f"values{j}", [P, J], F32)[:] for j in range(2)] + [kept[j][:, 0:J] for j in range(2, SLOTS)]
        roots = [sbuf(f"root{i}", [P, T], F32) for i in range(2)]
        recip = [sbuf(f"recip{i}", [P, T], F32) for i in range(SLOTS)]
        turned = [sbuf("turned", [P, T], F32), recip[1]]
        weights = [sbuf("first", [P, J], F32)[:], values[0], values[1], recip[1][:, J // 2 : J // 2 + J]]
        kept_halves = [[head[:, 3 * J // 2 : 5 * J // 2], weights[0]]] + [[kept[j][:, 0:BANK], kept[j][:, BANK:T]] for j in range(1, SLOTS)]
        y = sbuf("y", [P, 2, T], F32)
        y_bf = [sbuf(f"y_bf{h}", [P, SLOTS * T // QUARTERS], BF16) for h in range(QUARTERS)]
        y_w = sbuf("y_w", [P, T], U32)
        y_s = sbuf("y_s", [P, T], U8)

        def load_scales(plane, rows, quadrants=range(4)):
            words = rows[0].bitcast(I32)
            width = words.shape[1]
            for q in quadrants:
                nc.sync.dma_start(
                    out=plane[32 * q : 32 * q + 32, :].bitcast(I32),
                    in_=words[4 * q : 4 * q + 4, :].unsqueeze(0).to_broadcast([8, 4, width]),
                )

        def load_words(tile, words):
            nc.sync.dma_start(out=tile[:].bitcast(I32), in_=words.bitcast(I32))

        pr_rows = pr.rearrange("(p t) c -> p t c", t=SLOTS)
        old_rows = old.rearrange("(p t) c -> p t c", t=SLOTS)
        out_rows = out_0.rearrange("(p t) c -> p t c", t=SLOTS)

        def load_page_rows(j):
            nc.sync.dma_start(out=prior[j][:], in_=pr_rows[:, j, :])
            nc.sync.dma_start(out=state[j][:], in_=old_rows[:, j, :])

        load_scales(wb_s, wb_scales, range(0, 2))
        load_words(wb_w, wb_words[0].rearrange("p n t -> p (n t)"))
        load_words(xb_w, xb_words[0])
        load_scales(wb_s, wb_scales, range(2, 4))
        load_scales(xb_s, xb_scales)
        for h in range(2):
            nc.sync.dma_start(out=wa_raw[h][:], in_=wa.rearrange("(p i) (h n) -> p h i n", i=4, h=2)[:, h])
        load_words(xa_w, xa_words[0].rearrange("p n t -> p (n t)"))
        load_scales(xa_s, xa_scales)
        nc.sync.dma_start(offsets[:], offs)
        for j in range(SLOTS):
            load_page_rows(j)

        nc.vector.memset(zero[:], 0.0)
        nc.scalar.activation(one[:], zero[:], ACT.Exp)
        for page in den_pages:
            nc.vector.memset(page[:], 0.0)
        make_identity(nc, ident[:])
        nc.gpsimd.memset(num_page[:], 0.0)

        def cols(j):
            return slice(j * P, (j + 1) * P)

        def half(h):
            return slice(h * BANK, (h + 1) * BANK)

        def quarter(q):
            return slice(q * T // QUARTERS, (q + 1) * T // QUARTERS)

        for j in range(SLOTS):
            nc.vector.tensor_copy(out=wb_dw[:, cols(j)].bitcast(I32), in_=wb_w[:].bitcast(I32)[:, j::SLOTS])
            nc.vector.tensor_copy(out=wb_ds[:, cols(j)], in_=wb_s[:, j::SLOTS])
            nc.tensor.matmul_mx(
                out=u_banks[j][:],
                lhsT=wb_dw[:, cols(j)].bitcast(FP8X4),
                lhsT_scale=wb_ds[:, cols(j)],
                rhs=xb_w[:].bitcast(FP4X4),
                rhs_scale=xb_s[:],
                start=True,
                stop=True,
            )
        for j in range(SLOTS):
            nc.scalar.activation(expu[j], u_banks[j][:], ACT.Exp)

        def cap(j):
            nc.vector.tensor_scalar(capped[j][:], expu[j], EXP_CAP, None, ALU.min)

        def product(j):
            return capped[0][:] if j == 0 else roots[(j + 1) % 2][:, 0:J]


        def take_log(j):
            nc.scalar.activation(logs[j], capped[j][:], ACT.Ln, bias=one[:])

        def take_excess(j):
            nc.scalar.activation(excess[j - 1], u_banks[j][:], ACT.Relu, bias=-U_CAP)

        def weigh_old(j):
            if j == 0:
                for h in range(HALVES):
                    nc.gpsimd.tensor_tensor(kept_halves[0][h], prior[0][:, half(h)], state[0][:, half(h)], ALU.mult)
            else:
                nc.gpsimd.tensor_tensor(kept[j][:], prior[j][:], state[j][:], ALU.mult)

        def quantise_wa():
            for h in range(2):
                nc.vector.tensor_copy(
                    out=wa_bf.rearrange("p (t h m i) -> p h t m i", t=SLOTS, h=2, i=4)[:, h],
                    in_=wa_raw[h][:].rearrange("p i (m t) -> p t m i", t=SLOTS),
                )
            nc.vector.quantize_mx(out=wa_w[:].bitcast(FP8X4), scales=wa_s[:], in_=wa_bf)

        def make_values(j):
            nc.tensor.matmul_mx(
                out=v_bank[:],
                lhsT=wa_w[:, cols(j)].bitcast(FP8X4),
                lhsT_scale=wa_s[:, cols(j)],
                rhs=xa_w[:].bitcast(FP8X4),
                rhs_scale=xa_s[:],
                start=True,
                stop=True,
            )
            nc.scalar.copy(out=values[j], in_=v_bank[:])

        def weigh_values(j):
            nc.gpsimd.tensor_tensor(product(j), weights[j], values[j], ALU.mult)

        def turn(bank, src, start, stop):
            for b in range(BLOCKS):
                nc.tensor.matmul(
                    out=bank[:, cols(b)],
                    lhsT=src[:, cols(b)],
                    rhs=ident[:],
                    is_transpose=True,
                    start=start and b == 0,
                    stop=stop and b == BLOCKS - 1,
                )

        def open_sum(pair, first):
            for h in range(HALVES):
                turn(pair[h], first[h], True, False)

        def close_sum(pair, second):
            for h in range(HALVES):
                turn(pair[h], second[:, half(h)], False, True)

        def make_weights(j):
            if j == 0:
                nc.vector.tensor_tensor(weights[j], u_banks[j][:], logs[j], ALU.max)
            else:
                nc.gpsimd.tensor_tensor(weights[j], excess[j - 1], logs[j], ALU.add)

        def place_weights(j):
            nc.vector.tensor_copy(den_pages[j % 2][:].indirect(offsets[:]), weights[j])

        def take_roots(j):
            for h in range(HALVES):
                nc.scalar.activation(roots[j % 2][:, half(h)], den_banks[j][h][:], ACT.Abs_reciprocal_sqrt)

        def square_roots(j):
            for h in range(HALVES):
                nc.scalar.activation(recip[j][:, half(h)], roots[j % 2][:, half(h)], ACT.Square)

        def place_values(j):
            nc.vector.tensor_copy(num_page[:].indirect(offsets[:]), product(j))

        def divide_turned(j):
            for h in range(HALVES):
                nc.vector.tensor_tensor(turned[j // 2][:, half(h)], num_banks[h][:], recip[j][:, half(h)], ALU.mult)

        def turn_back(j):
            for h in range(HALVES):
                turn(y_banks[h], turned[j // 2][:, half(h)], True, True)
                nc.scalar.copy(out=y[:, j % 2, half(h)], in_=y_banks[h][:])
            nc.scalar.dma_start(out=out_rows[:, j, :], in_=y[:, j % 2, :])

        def weave(copy, pair, h):
            copy(
                out=y_bf[h][:].rearrange("p (c t) -> p c t", t=SLOTS)[:, :, 2 * pair : 2 * pair + 2].rearrange(
                    "p (c i) t -> p c t i", i=2
                ),
                in_=y[:, :, quarter(h)].rearrange("p t (c i) -> p c t i", i=2),
            )

        cap(0)
        take_log(0)
        make_weights(0)
        quantise_wa()
        for j in range(1, SLOTS):
            cap(j)
        place_weights(0)
        make_values(0)
        weigh_values(0)
        take_log(1)
        take_excess(1)
        place_values(0)
        make_weights(1)
        make_values(1)
        weigh_old(0)
        weigh_old(1)
        open_sum(den_banks[0], [prior[0][:, half(h)] for h in range(HALVES)])
        close_sum(den_banks[0], den_pages[0])
        place_weights(1)
        for j in range(2, SLOTS):
            take_log(j)
        for j in range(2, SLOTS):
            take_excess(j)
        take_roots(0)
        square_roots(0)
        make_values(2)
        open_sum(num_banks, kept_halves[0])
        close_sum(num_banks, num_page)
        open_sum(den_banks[1], [prior[1][:, half(h)] for h in range(HALVES)])
        make_values(3)
        weigh_values(1)
        make_weights(2)
        divide_turned(0)
        close_sum(den_banks[1], den_pages[1])
        take_roots(1)
        square_roots(1)
        turn_back(0)
        open_sum(num_banks, kept_halves[1])

        place_values(1)
        open_sum(den_banks[2], [prior[2][:, half(h)] for h in range(HALVES)])
        close_sum(num_banks, num_page)
        place_weights(2)
        weigh_values(2)
        weigh_old(2)
        divide_turned(1)
        make_weights(3)
        close_sum(den_banks[2], den_pages[0])
        take_roots(2)
        square_roots(2)
        turn_back(1)
        open_sum(num_banks, kept_halves[2])
        for q in range(QUARTERS):
            weave(nc.scalar.copy, 0, q)

        place_values(2)
        close_sum(num_banks, num_page)
        weigh_values(3)
        weigh_old(3)
        place_weights(3)
        divide_turned(2)
        for h in range(HALVES):
            nc.gpsimd.tensor_tensor(state[3][:, half(h)], prior[3][:, half(h)], den_pages[1][:, half(h)], ALU.add)
            nc.scalar.activation(y[:, 1, half(h)], state[3][:, half(h)], ACT.Abs_reciprocal_sqrt)
            nc.scalar.activation(recip[3][:, half(h)], y[:, 1, half(h)], ACT.Square)
        turn_back(2)

        last = SLOTS - 1
        place_values(last)
        words_out = out_1[0].rearrange("p c t -> p (c t)").bitcast(I32)
        for h in range(HALVES):
            for q in (2 * h, 2 * h + 1):
                nc.vector.tensor_tensor(
                    turned[0][:, quarter(q % 2)], num_page[:, quarter(q)], kept[last][:, quarter(q)], ALU.add
                )
            for q in (2 * h, 2 * h + 1):
                nc.vector.tensor_tensor(
                    y[:, last % 2, quarter(q)], turned[0][:, quarter(q % 2)], recip[last][:, quarter(q)], ALU.mult
                )
                weave(nc.scalar.copy if q < QUARTERS - 1 else nc.vector.tensor_copy, 1, q)
            nc.sync.dma_start(out=out_rows[:, last, half(h)], in_=y[:, last % 2, half(h)])
        for q in (0, 1, 3, 2):
            nc.vector.quantize_mx(out=y_w[:, quarter(q)].bitcast(FP8X4), scales=y_s[:, quarter(q)], in_=y_bf[q][:])
            if q in (1, 2):
                nc.sync.dma_start(out=words_out[:, half(q // 2)], in_=y_w[:, half(q // 2)].bitcast(I32))
        scales_out = out_2[0].bitcast(I32)
        for q in range(4):
            queue = nc.sync if q % 2 == 0 else nc.scalar
            queue.dma_start(out=scales_out[4 * q : 4 * q + 4, :], in_=y_s[32 * q : 32 * q + 4, :].bitcast(I32))
